import numpy as np
import ml_dtypes

BF16 = ml_dtypes.bfloat16


def bf(x):
    return np.asarray(x, np.float32).astype(BF16)


def f32(x):
    return np.asarray(x, np.float32)


def f64(x):
    return np.asarray(x).astype(np.float64)


def striped(idx):
    return np.tile(idx.reshape(-1, 16).T, (8, 1))


S, K, M, N, E, Q = 512, 256, 128, 256, 2, 128


def setup_inputs():
    return {"base": bf(np.random.standard_normal((M, S))), "x": bf(np.random.standard_normal((K, N))), "w": bf(np.random.standard_normal((E, K, M)) / np.sqrt(K)), "b": f32(0.5 * np.random.standard_normal((M, 1))), "offs": striped(np.random.permutation(S)[:N])}


def reference(base, x, w, b, offs):
    idx = offs[:16].T.reshape(-1)
    z = f64(base).copy()
    for e in range(E):
        z[:, idx[e * Q : (e + 1) * Q]] += f64(w)[e].T @ f64(x)[:, e * Q : (e + 1) * Q]
    return np.tanh(z + f64(b))

@@ -1,0 +1,58 @@
+import concourse.mybir as mybir
+from concourse.masks import make_identity
+
+BF16 = mybir.dt.bfloat16
+F32 = mybir.dt.float32
+U16 = mybir.dt.uint16
+TANH = mybir.ActivationFunctionType.Tanh
+
+P = 128
+TOKENS = 512
+CONTRACTION = 256
+EXPERTS = 2
+LISTED = 256
+PIECE = LISTED // EXPERTS
+K_BLOCKS = CONTRACTION // P
+OFFSETS_PER_COLUMN = 16
+
+FLOPS = 2 * CONTRACTION * P * LISTED
+
+
+def tile_scatter_matmul_kernel(tc, base, x, w, b, offs, out):
+    nc = tc.nc
+    with (
+        tc.tile_pool(name="sbuf", bufs=1) as sbuf,
+        tc.psum_pool(name="psum", bufs=1) as psum,
+    ):
+        base_tile = sbuf.tile([P, TOKENS], BF16)
+        x_tile = sbuf.tile([P, K_BLOCKS, LISTED], BF16)
+        w_tile = sbuf.tile([P, EXPERTS, K_BLOCKS, P], BF16)
+        offsets = sbuf.tile([P, LISTED // OFFSETS_PER_COLUMN], U16)
+        bias = sbuf.tile([P, 1], F32)
+        identity = sbuf.tile([P, P], BF16)
+        result = sbuf.tile([P, TOKENS], F32)
+        window = psum.tile([P, TOKENS], F32)
+
+        nc.sync.dma_start(base_tile[:], base)
+        nc.sync.dma_start(x_tile[:], x.rearrange("(p c) n -> p c n", c=K_BLOCKS))
+        nc.sync.dma_start(w_tile[:], w.rearrange("e (p c) m -> p e c m", c=K_BLOCKS))
+        nc.sync.dma_start(offsets[:], offs)
+        nc.sync.dma_start(bias[:], b)
+
+        make_identity(nc, identity[:])
+        nc.tensor.matmul(window[:], identity[:], base_tile[:], start=True, stop=False)
+
+        offset_columns = PIECE // OFFSETS_PER_COLUMN
+        for e in range(EXPERTS):
+            places = offsets[:, e * offset_columns : (e + 1) * offset_columns]
+            for c in range(K_BLOCKS):
+                nc.tensor.matmul(
+                    window[:].indirect(places),
+                    w_tile[:, e, c, :],
+                    x_tile[:, c, e * PIECE : (e + 1) * PIECE],
+                    start=False,
+                    stop=(e == EXPERTS - 1 and c == K_BLOCKS - 1),
+                )
+
+        nc.scalar.activation(result[:], window[:], TANH, bias=bias[:])
+        nc.sync.dma_start(out, result[:])

@@ -39,6 +39,10 @@ def tile_scatter_matmul_kernel(tc, base, x, w, b, offs, out):
         nc.sync.dma_start(offsets[:], offs)
         nc.sync.dma_start(bias[:], b)
 
+        early = sbuf.tile([P, 1], F32)
+        nc.vector.memset(early[:], 0.0)
+        nc.scalar.activation(early[:], early[:], TANH)
+
         make_identity(nc, identity[:])
         nc.tensor.matmul(window[:], identity[:], base_tile[:], start=True, stop=False)
 

@@ -14,6 +14,7 @@ LISTED = 256
 PIECE = LISTED // EXPERTS
 K_BLOCKS = CONTRACTION // P
 OFFSETS_PER_COLUMN = 16
+WARM_UPS = 12
 
 FLOPS = 2 * CONTRACTION * P * LISTED
 
@@ -39,9 +40,13 @@ def tile_scatter_matmul_kernel(tc, base, x, w, b, offs, out):
         nc.sync.dma_start(offsets[:], offs)
         nc.sync.dma_start(bias[:], b)
 
-        early = sbuf.tile([P, 1], F32)
-        nc.vector.memset(early[:], 0.0)
-        nc.scalar.activation(early[:], early[:], TANH)
+        zeros = sbuf.tile([P, P], BF16)
+        unread = sbuf.tile([P, 1], F32)
+        unread_bank = psum.tile([P, P], F32)
+        nc.vector.memset(zeros[:], 0.0)
+        nc.scalar.activation(unread[:], zeros[:, :1], TANH)
+        for turn in range(WARM_UPS):
+            nc.tensor.matmul(unread_bank[:], zeros[:], zeros[:], start=True, stop=True)
 
         make_identity(nc, identity[:])
         nc.tensor.matmul(window[:], identity[:], base_tile[:], start=True, stop=False)

import concourse.mybir as mybir
from concourse.masks import make_identity

BF16 = mybir.dt.bfloat16
F32 = mybir.dt.float32
U16 = mybir.dt.uint16
TANH = mybir.ActivationFunctionType.Tanh

P = 128
TOKENS = 512
CONTRACTION = 256
EXPERTS = 2
LISTED = 256
PIECE = LISTED // EXPERTS
K_BLOCKS = CONTRACTION // P
OFFSETS_PER_COLUMN = 16
WARM_UPS = 12

FLOPS = 2 * CONTRACTION * P * LISTED


def tile_scatter_matmul_kernel(tc, base, x, w, b, offs, out):
    nc = tc.nc
    with (
        tc.tile_pool(name="sbuf", bufs=1) as sbuf,
        tc.psum_pool(name="psum", bufs=1) as psum,
    ):
        base_tile = sbuf.tile([P, TOKENS], BF16)
        x_tile = sbuf.tile([P, K_BLOCKS, LISTED], BF16)
        w_tile = sbuf.tile([P, EXPERTS, K_BLOCKS, P], BF16)
        offsets = sbuf.tile([P, LISTED // OFFSETS_PER_COLUMN], U16)
        bias = sbuf.tile([P, 1], F32)
        identity = sbuf.tile([P, P], BF16)
        result = sbuf.tile([P, TOKENS], F32)
        window = psum.tile([P, TOKENS], F32)

        nc.sync.dma_start(base_tile[:], base)
        nc.sync.dma_start(x_tile[:], x.rearrange("(p c) n -> p c n", c=K_BLOCKS))
        nc.sync.dma_start(w_tile[:], w.rearrange("e (p c) m -> p e c m", c=K_BLOCKS))
        nc.sync.dma_start(offsets[:], offs)
        nc.sync.dma_start(bias[:], b)

        zeros = sbuf.tile([P, P], BF16)
        unread = sbuf.tile([P, 1], F32)
        unread_bank = psum.tile([P, P], F32)
        nc.vector.memset(zeros[:], 0.0)
        nc.scalar.activation(unread[:], zeros[:, :1], TANH)
        for turn in range(WARM_UPS):
            nc.tensor.matmul(unread_bank[:], zeros[:], zeros[:], start=True, stop=True)

        make_identity(nc, identity[:])
        nc.tensor.matmul(window[:], identity[:], base_tile[:], start=True, stop=False)

        offset_columns = PIECE // OFFSETS_PER_COLUMN
        for e in range(EXPERTS):
            places = offsets[:, e * offset_columns : (e + 1) * offset_columns]
            for c in range(K_BLOCKS):
                nc.tensor.matmul(
                    window[:].indirect(places),
                    w_tile[:, e, c, :],
                    x_tile[:, c, e * PIECE : (e + 1) * PIECE],
                    start=False,
                    stop=(e == EXPERTS - 1 and c == K_BLOCKS - 1),
                )

        nc.scalar.activation(result[:], window[:], TANH, bias=bias[:])
        nc.sync.dma_start(out, result[:])
